import numpy as np, ml_dtypes
CORES = [24,26,29,31,48,50,53,55]
N = 8
import mx_ref
NC = 128
BF = ml_dtypes.bfloat16
def cut(t, i, w=512):
    return t[:, w * i:w * i + w]
def term(a, B):
    return np.stack([np.maximum(mx_ref.matmul(mx_ref.quantize(cut(a, i)), B), 0) for i in range(4)], axis=2).reshape(128, -1)
def setup_inputs(rng):
    def f(*shape):
        return mx_ref.flush((rng.standard_normal(shape, dtype=np.float32) * np.exp2(rng.integers(-2, 3, shape[:-1] + (1,)))).astype(BF))
    return {"a": f(N, 128, 4 * 512), "b": f(N, 128, 4 * NC)}
def setup_inputs_blocks(rng):
    d = setup_inputs(rng)
    for k in ("a", "b"): d[k] = mx_ref.spread(d[k], rng, 2)
    return d
def setup_inputs_wide(rng):
    d = setup_inputs(rng)
    for k in ("a", "b"): d[k] = mx_ref.flush((d[k].astype(np.float32) * np.exp2(rng.integers(-4, 5, (N, 1, 1))).astype(np.float32)).astype(BF))
    return d
def setup_inputs_lossless(rng):
    a = np.zeros((N, 128, 4 * 128, 4), np.float32)
    for r in range(N):
        k = rng.integers(0, 512, size=4 * 128)
        a[r, k // 4, np.arange(4 * 128), k % 4] = 1.0
    size = np.repeat(2.0 ** rng.integers(-4, 5, size=(1, 1, (4 * NC) // 4)), 4, axis=2)
    b = (rng.random((N, 128, 4 * NC)) < 0.8) * size
    return {"a": a.reshape(N, 128, 4 * 512).astype(BF), "b": b.astype(np.float32).astype(BF)}
def reference(a, b):
    Bq = [mx_ref.quantize(b[c]) for c in range(N)]
    y = np.zeros((N, 128, 4 * NC), np.float32)
    for c in range(N):
        y[c] = mx_ref.total([term(a[r], Bq[c]) for r in range(N)])
    return {"y": y}

@@ -1,0 +1,220 @@
+from concourse.bass import DstId, RemoteDMATransfer
+from concourse.mybir import dt, AluOpType, ActivationFunctionType
+
+W = 128
+CODES = "float8_e4m3fn_x4"
+L = 4
+
+SCRATCH = {
+    "lda": ("sbuf", [128, 4 * L * W], "bfloat16"),
+    "ldb": ("sbuf", [128, 4 * W], "bfloat16"),
+    "aq": ("sbuf", [128, L * W], CODES), "ap": ("sbuf", [128, L * W], "uint8"),
+    "bq": ("sbuf", [128, L * W], CODES), "bp": ("sbuf", [128, L * W], "uint8"),
+    "rq": ("sbuf", [128, L * W], CODES), "rp": ("sbuf", [128, L * W], "uint8"),
+    "mq": ("sbuf", [128, L * W], CODES), "mp": ("sbuf", [128, L * W], "uint8"),
+    "eye": ("sbuf", [128, 4 * W + 4], "bfloat16"),
+    "sq": ("sbuf", [128, L * W], CODES), "sp": ("sbuf", [128, L * W], "uint8"),
+    "ho": ("sbuf", [128, 4 * L * W], "bfloat16"),
+    "hr": ("sbuf", [128, 4 * L * W], "bfloat16"),
+    "oq": ("sbuf", [128, L * W], CODES), "op": ("sbuf", [128, L * W], "uint8"),
+    "uq": ("sbuf", [128, L * W], CODES), "up": ("sbuf", [128, L * W], "uint8"),
+    "tq": ("sbuf", [128, 2 * L * W], CODES), "tp": ("sbuf", [128, 2 * L * W], "uint8"),
+    "hs": ("sbuf", [128, 4 * W], "float32"),
+    "ys": ("sbuf", [128, 4 * W], "float32"),
+    "pp": ("psum", [128, 512 * 4], "float32"),
+    "pu": ("psum", [128, 512 * 4], "float32"),
+}
+SEMAPHORES = (["lb", "la0", "la1", "ones", "eyed", "qb", "qa0", "qa1", "qs", "barr", "arem", "rlc", "rls", "sent",
+               "qo", "qr", "town", "hsd", "yd", "stored", "pr4", "rr4"]
+              + ["po%d" % i for i in range(4)] + ["ro%d" % i for i in range(4)]
+              + ["pr%d" % i for i in range(4)] + ["rr%d" % i for i in range(4)]
+              + ["tr%d" % i for i in range(4)] + ["un%d" % i for i in range(4)])
+
+
+def rank_program(g, core, T, topo):
+    if T.rank_of(core) is None:
+        return
+    chip = topo.chip(core)
+    mine = [c for c in T.cores if topo.chip(c) == chip]
+    far = [c for c in T.cores if topo.chip(c) != chip]
+    me = mine.index(core)
+    others = [l for l in range(len(mine)) if l != me]
+
+    def partner(c):
+        return far[mine.index(c)]
+
+    def port(c):
+        return topo.may_write(c, partner(c))
+
+    def via(c):
+        return [w for w in mine if topo.die(w) == topo.die(c) and topo.may_write(w, partner(c))][0]
+
+    def engines(src, dst):
+        m = topo.mask(src, dst)
+        return [1 << k for k in range(m.bit_length()) if m >> k & 1]
+
+    def did(c):
+        rid, pid, _ = topo.addr(c)
+        return DstId(rid=rid, pnc=pid)
+
+    sem = T.sem
+    sent = [0]
+
+    def send(out, in_, rsem, dst, bits):
+        rid, pid, _ = topo.addr(dst)
+        g.remote_dma(out, in_, rsem, sem.sent, pid, rid, sum(bits))
+        sent[0] += len(bits)
+
+    def cols(t, k, n=1):
+        return t[:, k * W:(k + n) * W]
+
+    def raw(t, k, n=1):
+        return t[:, k * W:(k + n) * W].bitcast(dt.uint8)
+
+    def bcast_bits(c):
+        return engines(c, partner(c)) if port(c) else engines(c, mine[(mine.index(c) + 1) % len(mine)])
+
+    def term_bits(s):
+        e = engines(s, mine[(mine.index(s) + 1) % len(mine)])
+        q = len(e) // 4
+        sets = [e[0:2 * q:2], e[2 * q::2]]
+        same = [e[1:2 * q:2], e[2 * q + 1::2]]
+        res = {}
+        for l, c in enumerate(mine):
+            if c != s:
+                pool = same if topo.die(c) == topo.die(s) else sets
+                res[l] = (pool or same).pop(0)
+        return res
+
+    g.sync.dma_start(T.ldb[:], T.b[:]).then_inc(sem.lb, 16)
+    h = 2 * L * W
+    g.scalar.dma_start(T.lda[:, 0:h], T.a[:, 0:h]).then_inc(sem.la0, 16)
+    g.sync.dma_start(T.lda[:, h:2 * h], T.a[:, h:2 * h]).then_inc(sem.la1, 16)
+
+    g.vector.memset(T.eye[:], 1.0).then_inc(sem.ones, 1)
+    g.wait_ge(sem.ones, 1)
+    g.affine_select(T.eye[:], T.eye[:], [[-1, 4 * W + 4]], AluOpType.is_equal, 0.0, 3, 4).then_inc(sem.eyed, 1)
+
+    v = g.vector
+    v.wait_ge(sem.lb, 16)
+    v.quantize_mx(cols(T.bq, me), cols(T.bp, me), T.ldb[:]).then_inc(sem.qb, 1)
+    v.wait_ge(sem.la0, 16)
+    v.quantize_mx(cols(T.aq, 0, 2), cols(T.ap, 0, 2), T.lda[:, 0:h]).then_inc(sem.qa0, 1)
+    v.wait_ge(sem.la1, 16)
+    v.quantize_mx(cols(T.aq, 2, 2), cols(T.ap, 2, 2), T.lda[:, h:2 * h]).then_inc(sem.qa1, 1)
+    v.wait_ge(sem.eyed, 1)
+    for b in range(L):
+        v.quantize_mx(cols(T.sq, b), cols(T.sp, b), T.eye[:, 3 - b:3 - b + 4 * W]).then_inc(sem.qs, 1)
+
+    def bcast(view_of, buf):
+        bits = bcast_bits(core)
+        g.remote_dma_fused([RemoteDMATransfer(dst_ids=[did(mine[l]) for l in others], dma_engine_mask=sum(bits),
+                                              remote_sem=sem.barr, srcs=[view_of(buf, me)],
+                                              dsts=[view_of(buf, me) for l in others])], local_sem=sem.sent)
+        sent[0] += len(bits)
+
+    g.wait_ge(sem.qb, 1)
+    bcast(raw, T.bq)
+    g.wait_ge(sem.qa0, 1)
+    g.wait_ge(sem.qa1, 1)
+    if port(core):
+        p = partner(core)
+        send(raw(T.mq, 0, L), raw(T.aq, 0, L), sem.arem, p, engines(core, p))
+        send(cols(T.mp, 0, L), cols(T.ap, 0, L), sem.arem, p, engines(core, p))
+    else:
+        w = via(core)
+        send(raw(T.rq, 0, L), raw(T.aq, 0, L), sem.rlc, w, engines(core, w))
+        send(cols(T.rp, 0, L), cols(T.ap, 0, L), sem.rls, w, engines(core, w))
+    bcast(cols, T.bp)
+
+    for s in mine:
+        if not port(s) and via(s) == core:
+            p, n = partner(s), len(engines(s, core))
+            g.wait_ge(sem.rlc, n)
+            send(raw(T.mq, 0, L), raw(T.rq, 0, L), sem.arem, p, engines(core, p))
+            g.wait_ge(sem.rls, n)
+            send(cols(T.mp, 0, L), cols(T.rp, 0, L), sem.arem, p, engines(core, p))
+
+    t = g.tensor
+    relu = ActivationFunctionType.Relu
+
+    def bank(ps, k, n=512):
+        return ps[:, 512 * k:512 * k + n]
+
+    def clamp(on, out, in_, s):
+        if on == 0:
+            g.scalar.activation(out, in_, relu).then_inc(s, 1)
+        else:
+            v.tensor_scalar(out, in_, 0.0, None, AluOpType.max).then_inc(s, 1)
+
+    t.wait_ge(sem.qb, 1)
+    t.wait_ge(sem.qa0, 1)
+    t.wait_ge(sem.qa1, 1)
+    t.wait_ge(sem.barr, sum(2 * len(bcast_bits(mine[l])) for l in others))
+    for i in range(L):
+        t.matmul_mx(bank(T.pp, i), cols(T.aq, i), cols(T.ap, i), cols(T.bq, 0, L), cols(T.bp, 0, L), True, True
+                    ).then_inc(sem["po%d" % i], 1)
+    for i in range(L):
+        q = (g.scalar, v)[i % 2]
+        q.wait_ge(sem["po%d" % i], 1)
+        clamp(i % 2, T.ho[:, i:4 * L * W:4], bank(T.pp, i), sem["ro%d" % i])
+    for i in range(L):
+        v.wait_ge(sem["ro%d" % i], 1)
+    for l in others:
+        v.quantize_mx(cols(T.oq, l), cols(T.op, l), T.ho[:, 4 * W * l:4 * W * (l + 1)]).then_inc(sem.qo, 1)
+
+    def scatter(view_of, src, dst, slot, rsem):
+        bits = term_bits(core)
+        g.remote_dma_fused([RemoteDMATransfer(dst_ids=[did(mine[l])], dma_engine_mask=sum(bits[l]), remote_sem=rsem,
+                                              srcs=[view_of(src, l)], dsts=[view_of(dst, slot)]) for l in others],
+                           local_sem=sem.sent)
+        sent[0] += sum(len(bits[l]) for l in others)
+
+    g.wait_ge(sem.qo, len(others))
+    scatter(raw, T.oq, T.tq, me, sem.town)
+    scatter(cols, T.op, T.tp, me, sem.town)
+
+    s_far = partner(core)
+    t.wait_ge(sem.arem, 2 * len(engines(s_far, core)))
+    parts = [(0, 0, 0, 4, 0), (1, 1, 0, 4, 1), (2, 2, 0, 4, 0), (3, 3, 0, 2, 1), (3, 0, 2, 2, 0)]
+    for k, (i, bk, lo, n, on) in enumerate(parts):
+        if k < 4:
+            t.wait_ge(sem["ro%d" % bk], 1)
+        else:
+            t.wait_ge(sem.rr0, 1)
+        t.matmul_mx(bank(T.pp, bk, n * W), cols(T.mq, i), cols(T.mp, i), cols(T.bq, lo, n), cols(T.bp, lo, n), True, True
+                    ).then_inc(sem["pr%d" % k], 1)
+        q = (g.scalar, v)[on]
+        q.wait_ge(sem["pr%d" % k], 1)
+        clamp(on, T.hr[:, 4 * W * lo + i:4 * W * (lo + n):4], bank(T.pp, bk, n * W), sem["rr%d" % k])
+    for k in range(len(parts)):
+        v.wait_ge(sem["rr%d" % k], 1)
+    for l in others:
+        v.quantize_mx(cols(T.uq, l), cols(T.up, l), T.hr[:, 4 * W * l:4 * W * (l + 1)]).then_inc(sem.qr, 1)
+    g.wait_ge(sem.qr, len(others))
+    scatter(raw, T.uq, T.tq, L + me, sem["tr%d" % me])
+    scatter(cols, T.up, T.tp, L + me, sem["tr%d" % me])
+    own = slice(4 * W * me, 4 * W * (me + 1))
+    v.tensor_tensor(T.hs[:], T.ho[:, own], T.hr[:, own], AluOpType.add).then_inc(sem.hsd, 1)
+
+    t.wait_ge(sem.qs, L)
+    t.wait_ge(sem.town, sum(2 * len(term_bits(mine[l])[me]) for l in others))
+    order = [(l, None) for l in others]
+    late = [l for l in others if port(mine[l])] + [l for l in others if not port(mine[l])]
+    order += [(L + l, l) for l in late]
+    for k, (slot, l) in enumerate(order):
+        if l is not None:
+            t.wait_ge(sem["tr%d" % l], 2 * len(term_bits(mine[l])[me]))
+        for b in range(L):
+            m = t.matmul_mx(bank(T.pu, b, W), cols(T.sq, b), cols(T.sp, b), cols(T.tq, slot), cols(T.tp, slot),
+                            k == 0, k == len(order) - 1)
+            if k == len(order) - 1:
+                m.then_inc(sem["un%d" % b], 1)
+    v.wait_ge(sem.hsd, 1)
+    for b in range(L):
+        v.wait_ge(sem["un%d" % b], 1)
+        v.tensor_tensor(T.ys[:, b:4 * W:4], bank(T.pu, b, W), T.hs[:, b:4 * W:4], AluOpType.add).then_inc(sem.yd, 1)
+    g.sync.wait_ge(sem.yd, L)
+    g.sync.dma_start(T.y[:], T.ys[:]).then_inc(sem.stored, 16)
+    g.sync.wait_ge(sem.stored, 16)
+    g.wait_ge(sem.sent, sent[0])

@@ -16,16 +16,21 @@ SCRATCH = {
     "sq": ("sbuf", [128, L * W], CODES), "sp": ("sbuf", [128, L * W], "uint8"),
     "ho": ("sbuf", [128, 4 * L * W], "bfloat16"),
     "hr": ("sbuf", [128, 4 * L * W], "bfloat16"),
+    "hs": ("sbuf", [128, 4 * W], "bfloat16"),
     "oq": ("sbuf", [128, L * W], CODES), "op": ("sbuf", [128, L * W], "uint8"),
     "uq": ("sbuf", [128, L * W], CODES), "up": ("sbuf", [128, L * W], "uint8"),
     "tq": ("sbuf", [128, 2 * L * W], CODES), "tp": ("sbuf", [128, 2 * L * W], "uint8"),
-    "hs": ("sbuf", [128, 4 * W], "float32"),
     "ys": ("sbuf", [128, 4 * W], "float32"),
     "pp": ("psum", [128, 512 * 4], "float32"),
     "pu": ("psum", [128, 512 * 4], "float32"),
 }
-SEMAPHORES = (["lb", "la0", "la1", "ones", "eyed", "qb", "qa0", "qa1", "qs", "barr", "arem", "rlc", "rls", "sent",
-               "qo", "qr", "town", "hsd", "yd", "stored", "pr4", "rr4"]
+FORWARDED = [(0, 2), None, (2, 1), (3, 1)]
+DIRECT = [(0, 4), None]
+SEND_FORWARDED = ["bq", 0, 1, "bp", 2, 3]
+SEND_DIRECT = ["bq", "bp", 0, 1]
+SEMAPHORES = (["lb", "la0", "la1", "ones", "eyed", "qb", "qa0", "qa1", "qs", "barr", "sent", "qo", "qr", "qself", "hsd",
+               "town", "yd", "stored", "pr4", "rr4"]
+              + ["m%d" % k for k in range(4)] + ["r%d" % k for k in range(4)]
               + ["po%d" % i for i in range(4)] + ["ro%d" % i for i in range(4)]
               + ["pr%d" % i for i in range(4)] + ["rr%d" % i for i in range(4)]
               + ["tr%d" % i for i in range(4)] + ["un%d" % i for i in range(4)])
@@ -39,6 +44,8 @@ def rank_program(g, core, T, topo):
     far = [c for c in T.cores if topo.chip(c) != chip]
     me = mine.index(core)
     others = [l for l in range(len(mine)) if l != me]
+    sem = T.sem
+    sent = [0]
 
     def partner(c):
         return far[mine.index(c)]
@@ -57,11 +64,9 @@ def rank_program(g, core, T, topo):
         rid, pid, _ = topo.addr(c)
         return DstId(rid=rid, pnc=pid)
 
-    sem = T.sem
-    sent = [0]
-
-    def send(out, in_, rsem, dst, bits):
+    def send(out, in_, rsem, dst):
         rid, pid, _ = topo.addr(dst)
+        bits = engines(core, dst)
         g.remote_dma(out, in_, rsem, sem.sent, pid, rid, sum(bits))
         sent[0] += len(bits)
 
@@ -71,20 +76,19 @@ def rank_program(g, core, T, topo):
     def raw(t, k, n=1):
         return t[:, k * W:(k + n) * W].bitcast(dt.uint8)
 
+    def chunk(q, p, x):
+        return cols(p, 0, L) if x is None else raw(q, x[0], x[1])
+
     def bcast_bits(c):
-        return engines(c, partner(c)) if port(c) else engines(c, mine[(mine.index(c) + 1) % len(mine)])
+        e = engines(c, mine[(mine.index(c) + 1) % len(mine)])
+        return [k for k in e if k not in engines(c, partner(c))] if port(c) else e
 
     def term_bits(s):
         e = engines(s, mine[(mine.index(s) + 1) % len(mine)])
-        q = len(e) // 4
-        sets = [e[0:2 * q:2], e[2 * q::2]]
-        same = [e[1:2 * q:2], e[2 * q + 1::2]]
-        res = {}
-        for l, c in enumerate(mine):
-            if c != s:
-                pool = same if topo.die(c) == topo.die(s) else sets
-                res[l] = (pool or same).pop(0)
-        return res
+        q = len(e) // 2
+        away = [e[0:q:2], e[q::2]]
+        same = [e[1:q:2]]
+        return {l: (same if topo.die(c) == topo.die(s) else away).pop(0) for l, c in enumerate(mine) if c != s}
 
     g.sync.dma_start(T.ldb[:], T.b[:]).then_inc(sem.lb, 16)
     h = 2 * L * W
@@ -114,26 +118,33 @@ def rank_program(g, core, T, topo):
         sent[0] += len(bits)
 
     g.wait_ge(sem.qb, 1)
-    bcast(raw, T.bq)
-    g.wait_ge(sem.qa0, 1)
-    g.wait_ge(sem.qa1, 1)
-    if port(core):
-        p = partner(core)
-        send(raw(T.mq, 0, L), raw(T.aq, 0, L), sem.arem, p, engines(core, p))
-        send(cols(T.mp, 0, L), cols(T.ap, 0, L), sem.arem, p, engines(core, p))
-    else:
-        w = via(core)
-        send(raw(T.rq, 0, L), raw(T.aq, 0, L), sem.rlc, w, engines(core, w))
-        send(cols(T.rp, 0, L), cols(T.ap, 0, L), sem.rls, w, engines(core, w))
-    bcast(cols, T.bp)
+    ready = []
+
+    def need(x):
+        if x not in ready:
+            g.wait_ge(sem[x], 1)
+            ready.append(x)
+
+    for step in (SEND_DIRECT if port(core) else SEND_FORWARDED):
+        if step == "bp":
+            bcast(cols, T.bp)
+        elif step == "bq":
+            bcast(raw, T.bq)
+        else:
+            x = (DIRECT if port(core) else FORWARDED)[step]
+            need("qa0")
+            if x is None or x[0] + x[1] > 2:
+                need("qa1")
+            if port(core):
+                send(chunk(T.mq, T.mp, x), chunk(T.aq, T.ap, x), sem["m%d" % step], partner(core))
+            else:
+                send(chunk(T.rq, T.rp, x), chunk(T.aq, T.ap, x), sem["r%d" % step], via(core))
 
     for s in mine:
         if not port(s) and via(s) == core:
-            p, n = partner(s), len(engines(s, core))
-            g.wait_ge(sem.rlc, n)
-            send(raw(T.mq, 0, L), raw(T.rq, 0, L), sem.arem, p, engines(core, p))
-            g.wait_ge(sem.rls, n)
-            send(cols(T.mp, 0, L), cols(T.rp, 0, L), sem.arem, p, engines(core, p))
+            for k, x in enumerate(FORWARDED):
+                g.wait_ge(sem["r%d" % k], len(engines(s, core)))
+                send(chunk(T.mq, T.mp, x), chunk(T.rq, T.rp, x), sem["m%d" % k], partner(s))
 
     t = g.tensor
     relu = ActivationFunctionType.Relu
@@ -160,8 +171,12 @@ def rank_program(g, core, T, topo):
         clamp(i % 2, T.ho[:, i:4 * L * W:4], bank(T.pp, i), sem["ro%d" % i])
     for i in range(L):
         v.wait_ge(sem["ro%d" % i], 1)
+
+    def share(src, l):
+        return src[:, 4 * W * l:4 * W * (l + 1)]
+
     for l in others:
-        v.quantize_mx(cols(T.oq, l), cols(T.op, l), T.ho[:, 4 * W * l:4 * W * (l + 1)]).then_inc(sem.qo, 1)
+        v.quantize_mx(cols(T.oq, l), cols(T.op, l), share(T.ho, l)).then_inc(sem.qo, 1)
 
     def scatter(view_of, src, dst, slot, rsem):
         bits = term_bits(core)
@@ -175,45 +190,58 @@ def rank_program(g, core, T, topo):
     scatter(cols, T.op, T.tp, me, sem.town)
 
     s_far = partner(core)
-    t.wait_ge(sem.arem, 2 * len(engines(s_far, core)))
-    parts = [(0, 0, 0, 4, 0), (1, 1, 0, 4, 1), (2, 2, 0, 4, 0), (3, 3, 0, 2, 1), (3, 0, 2, 2, 0)]
+    kinds = DIRECT if topo.may_write(s_far, core) else FORWARDED
+    n_far = len(engines(s_far, core))
+    planes = kinds.index(None)
+    holds = {i: k for k, x in enumerate(kinds) if x is not None for i in range(x[0], x[0] + x[1])}
+    got = [planes]
+    t.wait_ge(sem["m%d" % planes], n_far)
+    a, c = (0, 2) if me >= 2 else (2, 0)
+    parts = [(0, 0, 0, 4, 0), (1, 1, 0, 4, 1), (2, 2, 0, 4, 0), (3, 3, a, 2, 1), (3, 0, c, 2, 0)]
     for k, (i, bk, lo, n, on) in enumerate(parts):
-        if k < 4:
-            t.wait_ge(sem["ro%d" % bk], 1)
-        else:
-            t.wait_ge(sem.rr0, 1)
+        if holds[i] not in got:
+            t.wait_ge(sem["m%d" % holds[i]], n_far)
+            got.append(holds[i])
+        t.wait_ge(sem["ro%d" % bk] if k < 4 else sem.rr0, 1)
         t.matmul_mx(bank(T.pp, bk, n * W), cols(T.mq, i), cols(T.mp, i), cols(T.bq, lo, n), cols(T.bp, lo, n), True, True
                     ).then_inc(sem["pr%d" % k], 1)
         q = (g.scalar, v)[on]
         q.wait_ge(sem["pr%d" % k], 1)
         clamp(on, T.hr[:, 4 * W * lo + i:4 * W * (lo + n):4], bank(T.pp, bk, n * W), sem["rr%d" % k])
-    for k in range(len(parts)):
+    for k in range(len(parts) - 1):
         v.wait_ge(sem["rr%d" % k], 1)
-    for l in others:
-        v.quantize_mx(cols(T.uq, l), cols(T.up, l), T.hr[:, 4 * W * l:4 * W * (l + 1)]).then_inc(sem.qr, 1)
+    for l in (a, a + 1, c, c + 1):
+        if l == c:
+            v.wait_ge(sem.rr4, 1)
+        if l != me:
+            v.quantize_mx(cols(T.uq, l), cols(T.up, l), share(T.hr, l)).then_inc(sem.qr, 1)
     g.wait_ge(sem.qr, len(others))
     scatter(raw, T.uq, T.tq, L + me, sem["tr%d" % me])
     scatter(cols, T.up, T.tp, L + me, sem["tr%d" % me])
-    own = slice(4 * W * me, 4 * W * (me + 1))
-    v.tensor_tensor(T.hs[:], T.ho[:, own], T.hr[:, own], AluOpType.add).then_inc(sem.hsd, 1)
+    v.tensor_tensor(T.hs[:], share(T.ho, me), share(T.hr, me), AluOpType.add).then_inc(sem.hsd, 1)
+    v.wait_ge(sem.hsd, 1)
+    v.quantize_mx(cols(T.oq, me), cols(T.op, me), T.hs[:]).then_inc(sem.qself, 1)
 
     t.wait_ge(sem.qs, L)
-    t.wait_ge(sem.town, sum(2 * len(term_bits(mine[l])[me]) for l in others))
-    order = [(l, None) for l in others]
+    tq = [(T.tq, T.tp, l, sem.town, sum(2 * len(term_bits(mine[x])[me]) for x in others)) for l in others]
+    tq += [(T.oq, T.op, me, sem.qself, 1)]
     late = [l for l in others if port(mine[l])] + [l for l in others if not port(mine[l])]
-    order += [(L + l, l) for l in late]
-    for k, (slot, l) in enumerate(order):
-        if l is not None:
-            t.wait_ge(sem["tr%d" % l], 2 * len(term_bits(mine[l])[me]))
+    tq += [(T.tq, T.tp, L + l, sem["tr%d" % l], 2 * len(term_bits(mine[l])[me])) for l in late]
+    for k, (cq, cp, slot, s, n) in enumerate(tq):
+        t.wait_ge(s, n)
         for b in range(L):
-            m = t.matmul_mx(bank(T.pu, b, W), cols(T.sq, b), cols(T.sp, b), cols(T.tq, slot), cols(T.tp, slot),
-                            k == 0, k == len(order) - 1)
-            if k == len(order) - 1:
+            m = t.matmul_mx(bank(T.pu, b, W), cols(T.sq, b), cols(T.sp, b), cols(cq, slot), cols(cp, slot),
+                            k == 0, k == len(tq) - 1)
+            if k == len(tq) - 1:
                 m.then_inc(sem["un%d" % b], 1)
-    v.wait_ge(sem.hsd, 1)
+
     for b in range(L):
-        v.wait_ge(sem["un%d" % b], 1)
-        v.tensor_tensor(T.ys[:, b:4 * W:4], bank(T.pu, b, W), T.hs[:, b:4 * W:4], AluOpType.add).then_inc(sem.yd, 1)
+        q = (g.scalar, v)[b % 2]
+        q.wait_ge(sem["un%d" % b], 1)
+        if b % 2:
+            v.tensor_copy(T.ys[:, b:4 * W:4], bank(T.pu, b, W)).then_inc(sem.yd, 1)
+        else:
+            g.scalar.activation(T.ys[:, b:4 * W:4], bank(T.pu, b, W), ActivationFunctionType.Copy).then_inc(sem.yd, 1)
     g.sync.wait_ge(sem.yd, L)
     g.sync.dma_start(T.y[:], T.ys[:]).then_inc(sem.stored, 16)
     g.sync.wait_ge(sem.stored, 16)

@@ -4,48 +4,57 @@ from concourse.mybir import dt, AluOpType, ActivationFunctionType
 W = 128
 CODES = "float8_e4m3fn_x4"
 L = 4
+B = 4 * W
+SIM = 64
 
 SCRATCH = {
-    "lda": ("sbuf", [128, 4 * L * W], "bfloat16"),
-    "ldb": ("sbuf", [128, 4 * W], "bfloat16"),
+    "lda": ("sbuf", [128, B * L], "bfloat16"),
+    "ldb": ("sbuf", [128, B], "bfloat16"),
     "aq": ("sbuf", [128, L * W], CODES), "ap": ("sbuf", [128, L * W], "uint8"),
     "bq": ("sbuf", [128, L * W], CODES), "bp": ("sbuf", [128, L * W], "uint8"),
     "rq": ("sbuf", [128, L * W], CODES), "rp": ("sbuf", [128, L * W], "uint8"),
     "mq": ("sbuf", [128, L * W], CODES), "mp": ("sbuf", [128, L * W], "uint8"),
-    "eye": ("sbuf", [128, 4 * W + 4], "bfloat16"),
+    "one": ("sbuf", [128, W], "bfloat16"),
+    "eye": ("sbuf", [128, B + 4], "bfloat16"),
     "sq": ("sbuf", [128, L * W], CODES), "sp": ("sbuf", [128, L * W], "uint8"),
-    "ho": ("sbuf", [128, 4 * L * W], "bfloat16"),
-    "hr": ("sbuf", [128, 4 * L * W], "bfloat16"),
-    "hs": ("sbuf", [128, 4 * W], "bfloat16"),
+    "ho": ("sbuf", [128, B * L], "bfloat16"),
+    "hr": ("sbuf", [128, B * L], "bfloat16"),
+    "hs": ("sbuf", [128, B], "bfloat16"),
     "oq": ("sbuf", [128, L * W], CODES), "op": ("sbuf", [128, L * W], "uint8"),
     "uq": ("sbuf", [128, L * W], CODES), "up": ("sbuf", [128, L * W], "uint8"),
     "tq": ("sbuf", [128, 2 * L * W], CODES), "tp": ("sbuf", [128, 2 * L * W], "uint8"),
-    "ys": ("sbuf", [128, 4 * W], "float32"),
+    "ys": ("sbuf", [128, B], "float32"),
     "pp": ("psum", [128, 512 * 4], "float32"),
     "pu": ("psum", [128, 512 * 4], "float32"),
 }
-FORWARDED = [(0, 2), None, (2, 1), (3, 1)]
-DIRECT = [(0, 4), None]
-SEND_FORWARDED = ["bq", 0, 1, "bp", 2, 3]
-SEND_DIRECT = ["bq", "bp", 0, 1]
-SEMAPHORES = (["lb", "la0", "la1", "ones", "eyed", "qb", "qa0", "qa1", "qs", "barr", "sent", "qo", "qr", "qself", "hsd",
-               "town", "yd", "stored", "pr4", "rr4"]
-              + ["m%d" % k for k in range(4)] + ["r%d" % k for k in range(4)]
-              + ["po%d" % i for i in range(4)] + ["ro%d" % i for i in range(4)]
-              + ["pr%d" % i for i in range(4)] + ["rr%d" % i for i in range(4)]
-              + ["tr%d" % i for i in range(4)] + ["un%d" % i for i in range(4)])
+FORWARDED = [(0, 1, "plane"), (1, 1, "plane"), (None, 0, "rank"), (2, 1, "rank"), (3, 1, "plane")]
+DIRECT = [(0, 2, None), (2, 2, None), (None, 0, None)]
+SEND_FORWARDED = ["bq", 0, 1, 2, "bp", 3, 4]
+SEND_DIRECT = ["bq", 0, "bp", 1, 2]
+SEMAPHORES = (["lb", "la0", "la1", "ones", "zero", "diag", "eyed", "qb", "qa0", "qa1", "qs", "barr", "sent", "qo", "qr",
+               "qself", "hsd", "town", "yd", "stored", "pr4", "rr4"]
+              + ["m%d" % k for k in range(5)] + ["r%d" % k for k in range(5)]
+              + [p + "%d" % i for p in ("po", "ro", "ps", "rs", "pr", "rr", "pt", "rt", "tr", "un") for i in range(4)])
 
 
 def rank_program(g, core, T, topo):
-    if T.rank_of(core) is None:
-        return
+    homes = sorted({topo.chip(c) for c in T.cores})
     chip = topo.chip(core)
+    if chip not in homes:
+        homes = [x for x in homes if topo.same_plane(x, chip)] + [x for x in homes if topo.mates(x, chip)]
+        if len(homes) < 2:
+            return
+        chip = homes[0]
     mine = [c for c in T.cores if topo.chip(c) == chip]
     far = [c for c in T.cores if topo.chip(c) != chip]
-    me = mine.index(core)
-    others = [l for l in range(len(mine)) if l != me]
     sem = T.sem
     sent = [0]
+
+    def rest(c):
+        return [x for x in mine if x != c]
+
+    def slot(d, s):
+        return 0 if s == d else 1 + rest(d).index(s)
 
     def partner(c):
         return far[mine.index(c)]
@@ -53,8 +62,14 @@ def rank_program(g, core, T, topo):
     def port(c):
         return topo.may_write(c, partner(c))
 
-    def via(c):
-        return [w for w in mine if topo.die(w) == topo.die(c) and topo.may_write(w, partner(c))][0]
+    def via(c, way):
+        own = [w for w in range(SIM) if topo.die(w) == topo.die(c) and topo.may_write(w, partner(c))]
+        if way == "rank":
+            return [w for w in own if w in mine][0]
+        return [w for w in own if topo.same_plane(topo.chip(w), chip) and topo.mates(topo.chip(w), topo.chip(far[0]))][0]
+
+    def chunks(c):
+        return DIRECT if port(c) else FORWARDED
 
     def engines(src, dst):
         m = topo.mask(src, dst)
@@ -77,44 +92,60 @@ def rank_program(g, core, T, topo):
         return t[:, k * W:(k + n) * W].bitcast(dt.uint8)
 
     def chunk(q, p, x):
-        return cols(p, 0, L) if x is None else raw(q, x[0], x[1])
+        return cols(p, 0, L) if x[0] is None else raw(q, x[0], x[1])
 
     def bcast_bits(c):
-        e = engines(c, mine[(mine.index(c) + 1) % len(mine)])
-        return [k for k in e if k not in engines(c, partner(c))] if port(c) else e
+        return [k for k in engines(c, rest(c)[0]) if k not in engines(c, partner(c))]
 
     def term_bits(s):
-        e = engines(s, mine[(mine.index(s) + 1) % len(mine)])
+        e = engines(s, rest(s)[0])
         q = len(e) // 2
         away = [e[0:q:2], e[q::2]]
-        same = [e[1:q:2]]
-        return {l: (same if topo.die(c) == topo.die(s) else away).pop(0) for l, c in enumerate(mine) if c != s}
+        return {c: e[1::2] if topo.die(c) == topo.die(s) else away.pop(0) for c in rest(s)}
 
+    def forward():
+        for s in mine:
+            for k, x in enumerate(chunks(s)):
+                if x[2] is not None and via(s, x[2]) == core:
+                    g.wait_ge(sem["r%d" % k], len(engines(s, core)))
+                    send(chunk(T.mq, T.mp, x), chunk(T.rq, T.rp, x), sem["m%d" % k], partner(s))
+
+    if core not in mine:
+        forward()
+        if sent[0]:
+            g.wait_ge(sem.sent, sent[0])
+        return
+
+    h = B * L // 2
     g.sync.dma_start(T.ldb[:], T.b[:]).then_inc(sem.lb, 16)
-    h = 2 * L * W
-    g.scalar.dma_start(T.lda[:, 0:h], T.a[:, 0:h]).then_inc(sem.la0, 16)
+    g.sync.dma_start(T.lda[:, 0:h], T.a[:, 0:h]).then_inc(sem.la0, 16)
     g.sync.dma_start(T.lda[:, h:2 * h], T.a[:, h:2 * h]).then_inc(sem.la1, 16)
 
-    g.vector.memset(T.eye[:], 1.0).then_inc(sem.ones, 1)
-    g.wait_ge(sem.ones, 1)
-    g.affine_select(T.eye[:], T.eye[:], [[-1, 4 * W + 4]], AluOpType.is_equal, 0.0, 3, 4).then_inc(sem.eyed, 1)
-
     v = g.vector
+    v.memset(T.one[:], 1.0).then_inc(sem.ones, 1)
+    v.memset(T.eye[:], 0.0).then_inc(sem.zero, 1)
+    g.wait_ge(sem.ones, 1)
+    g.affine_select(T.one[:], T.one[:], [[-1, W]], AluOpType.is_equal, 0.0, 0, 1).then_inc(sem.diag, 1)
+    v.wait_ge(sem.diag, 1)
+    v.wait_ge(sem.zero, 1)
+    v.tensor_copy(T.eye[:, 3:3 + B:4], T.one[:]).then_inc(sem.eyed, 1)
+
     v.wait_ge(sem.lb, 16)
-    v.quantize_mx(cols(T.bq, me), cols(T.bp, me), T.ldb[:]).then_inc(sem.qb, 1)
+    v.quantize_mx(cols(T.bq, 0), cols(T.bp, 0), T.ldb[:]).then_inc(sem.qb, 1)
     v.wait_ge(sem.la0, 16)
     v.quantize_mx(cols(T.aq, 0, 2), cols(T.ap, 0, 2), T.lda[:, 0:h]).then_inc(sem.qa0, 1)
     v.wait_ge(sem.la1, 16)
     v.quantize_mx(cols(T.aq, 2, 2), cols(T.ap, 2, 2), T.lda[:, h:2 * h]).then_inc(sem.qa1, 1)
     v.wait_ge(sem.eyed, 1)
     for b in range(L):
-        v.quantize_mx(cols(T.sq, b), cols(T.sp, b), T.eye[:, 3 - b:3 - b + 4 * W]).then_inc(sem.qs, 1)
+        v.quantize_mx(cols(T.sq, b), cols(T.sp, b), T.eye[:, 3 - b:3 - b + B]).then_inc(sem.qs, 1)
 
     def bcast(view_of, buf):
         bits = bcast_bits(core)
-        g.remote_dma_fused([RemoteDMATransfer(dst_ids=[did(mine[l]) for l in others], dma_engine_mask=sum(bits),
-                                              remote_sem=sem.barr, srcs=[view_of(buf, me)],
-                                              dsts=[view_of(buf, me) for l in others])], local_sem=sem.sent)
+        g.remote_dma_fused([RemoteDMATransfer(dst_ids=[did(c) for c in rest(core)], dma_engine_mask=sum(bits),
+                                              remote_sem=sem.barr, srcs=[view_of(buf, 0)],
+                                              dsts=[view_of(buf, slot(c, core)) for c in rest(core)])],
+                           local_sem=sem.sent)
         sent[0] += len(bits)
 
     g.wait_ge(sem.qb, 1)
@@ -131,117 +162,124 @@ def rank_program(g, core, T, topo):
         elif step == "bq":
             bcast(raw, T.bq)
         else:
-            x = (DIRECT if port(core) else FORWARDED)[step]
-            need("qa0")
-            if x is None or x[0] + x[1] > 2:
+            x = chunks(core)[step]
+            if x[0] is None or x[0] < 2:
+                need("qa0")
+            if x[0] is None or x[0] + x[1] > 2:
                 need("qa1")
-            if port(core):
+            if x[2] is None:
                 send(chunk(T.mq, T.mp, x), chunk(T.aq, T.ap, x), sem["m%d" % step], partner(core))
             else:
-                send(chunk(T.rq, T.rp, x), chunk(T.aq, T.ap, x), sem["r%d" % step], via(core))
-
-    for s in mine:
-        if not port(s) and via(s) == core:
-            for k, x in enumerate(FORWARDED):
-                g.wait_ge(sem["r%d" % k], len(engines(s, core)))
-                send(chunk(T.mq, T.mp, x), chunk(T.rq, T.rp, x), sem["m%d" % k], partner(s))
+                send(chunk(T.rq, T.rp, x), chunk(T.aq, T.ap, x), sem["r%d" % step], via(core, x[2]))
+    forward()
 
     t = g.tensor
-    relu = ActivationFunctionType.Relu
 
-    def bank(ps, k, n=512):
-        return ps[:, 512 * k:512 * k + n]
+    def bank(ps, k, n):
+        return ps[:, 512 * k:512 * k + n * W]
 
-    def clamp(on, out, in_, s):
+    def product(q, p, i, lo, n, bk, done):
+        t.matmul_mx(bank(T.pp, bk, n), cols(q, i), cols(p, i), cols(T.bq, lo, n), cols(T.bp, lo, n), True, True
+                    ).then_inc(sem[done], 1)
+
+    def clamp(on, h, i, lo, n, bk, after, done):
+        (g.scalar, v)[on].wait_ge(sem[after], 1)
+        out, in_ = h[:, B * lo + i:B * (lo + n):4], bank(T.pp, bk, n)
         if on == 0:
-            g.scalar.activation(out, in_, relu).then_inc(s, 1)
+            g.scalar.activation(out, in_, ActivationFunctionType.Relu).then_inc(sem[done], 1)
         else:
-            v.tensor_scalar(out, in_, 0.0, None, AluOpType.max).then_inc(s, 1)
+            v.tensor_scalar(out, in_, 0.0, None, AluOpType.max).then_inc(sem[done], 1)
 
+    def pack(q, p, h, k, s):
+        v.quantize_mx(cols(q, k), cols(p, k), h[:, B * k:B * (k + 1)]).then_inc(sem[s], 1)
+
+    def scatter(view_of, src, dst, base, rsem):
+        bits = term_bits(core)
+        g.remote_dma_fused([RemoteDMATransfer(dst_ids=[did(c)], dma_engine_mask=sum(bits[c]), remote_sem=sem[rsem(c)],
+                                              srcs=[view_of(src, slot(core, c))],
+                                              dsts=[view_of(dst, base + slot(c, core))]) for c in rest(core)],
+                           local_sem=sem.sent)
+        sent[0] += sum(len(bits[c]) for c in rest(core))
+
+    m = L - 1
     t.wait_ge(sem.qb, 1)
     t.wait_ge(sem.qa0, 1)
-    t.wait_ge(sem.qa1, 1)
-    t.wait_ge(sem.barr, sum(2 * len(bcast_bits(mine[l])) for l in others))
     for i in range(L):
-        t.matmul_mx(bank(T.pp, i), cols(T.aq, i), cols(T.ap, i), cols(T.bq, 0, L), cols(T.bp, 0, L), True, True
-                    ).then_inc(sem["po%d" % i], 1)
+        if i == 2:
+            t.wait_ge(sem.qa1, 1)
+        product(T.aq, T.ap, i, 0, 1, i, "ps%d" % i)
+        clamp(0, T.ho, i, 0, 1, i, "ps%d" % i, "rs%d" % i)
+    t.wait_ge(sem.barr, sum(2 * len(bcast_bits(c)) for c in rest(core)))
     for i in range(L):
-        q = (g.scalar, v)[i % 2]
-        q.wait_ge(sem["po%d" % i], 1)
-        clamp(i % 2, T.ho[:, i:4 * L * W:4], bank(T.pp, i), sem["ro%d" % i])
+        t.wait_ge(sem["rs%d" % i], 1)
+        product(T.aq, T.ap, i, 1, m, i, "po%d" % i)
+        clamp(i % 2, T.ho, i, 1, m, i, "po%d" % i, "ro%d" % i)
     for i in range(L):
         v.wait_ge(sem["ro%d" % i], 1)
-
-    def share(src, l):
-        return src[:, 4 * W * l:4 * W * (l + 1)]
-
-    for l in others:
-        v.quantize_mx(cols(T.oq, l), cols(T.op, l), share(T.ho, l)).then_inc(sem.qo, 1)
-
-    def scatter(view_of, src, dst, slot, rsem):
-        bits = term_bits(core)
-        g.remote_dma_fused([RemoteDMATransfer(dst_ids=[did(mine[l])], dma_engine_mask=sum(bits[l]), remote_sem=rsem,
-                                              srcs=[view_of(src, l)], dsts=[view_of(dst, slot)]) for l in others],
-                           local_sem=sem.sent)
-        sent[0] += sum(len(bits[l]) for l in others)
-
-    g.wait_ge(sem.qo, len(others))
-    scatter(raw, T.oq, T.tq, me, sem.town)
-    scatter(cols, T.op, T.tp, me, sem.town)
+    for k in range(1, L):
+        pack(T.oq, T.op, T.ho, k, "qo")
+    g.wait_ge(sem.qo, m)
+    scatter(raw, T.oq, T.tq, 0, lambda c: "town")
+    scatter(cols, T.op, T.tp, 0, lambda c: "town")
 
     s_far = partner(core)
     kinds = DIRECT if topo.may_write(s_far, core) else FORWARDED
     n_far = len(engines(s_far, core))
-    planes = kinds.index(None)
-    holds = {i: k for k, x in enumerate(kinds) if x is not None for i in range(x[0], x[0] + x[1])}
-    got = [planes]
-    t.wait_ge(sem["m%d" % planes], n_far)
-    a, c = (0, 2) if me >= 2 else (2, 0)
-    parts = [(0, 0, 0, 4, 0), (1, 1, 0, 4, 1), (2, 2, 0, 4, 0), (3, 3, a, 2, 1), (3, 0, c, 2, 0)]
-    for k, (i, bk, lo, n, on) in enumerate(parts):
-        if holds[i] not in got:
-            t.wait_ge(sem["m%d" % holds[i]], n_far)
-            got.append(holds[i])
+    got = []
+
+    def arrived(k):
+        if k not in got:
+            t.wait_ge(sem["m%d" % k], n_far)
+            got.append(k)
+
+    holds = {i: k for k, x in enumerate(kinds) if x[0] is not None for i in range(x[0], x[0] + x[1])}
+    arrived([k for k, x in enumerate(kinds) if x[0] is None][0])
+    for k, (i, bk, lo, n, on) in enumerate([(0, 0, 1, m, 0), (1, 1, 1, m, 1), (2, 2, 1, m, 0), (3, 3, 1, 2, 1), (3, 0, 3, 1, 0)]):
+        arrived(holds[i])
         t.wait_ge(sem["ro%d" % bk] if k < 4 else sem.rr0, 1)
-        t.matmul_mx(bank(T.pp, bk, n * W), cols(T.mq, i), cols(T.mp, i), cols(T.bq, lo, n), cols(T.bp, lo, n), True, True
-                    ).then_inc(sem["pr%d" % k], 1)
-        q = (g.scalar, v)[on]
-        q.wait_ge(sem["pr%d" % k], 1)
-        clamp(on, T.hr[:, 4 * W * lo + i:4 * W * (lo + n):4], bank(T.pp, bk, n * W), sem["rr%d" % k])
-    for k in range(len(parts) - 1):
+        product(T.mq, T.mp, i, lo, n, bk, "pr%d" % k)
+        clamp(on, T.hr, i, lo, n, bk, "pr%d" % k, "rr%d" % k)
+    for k in range(4):
         v.wait_ge(sem["rr%d" % k], 1)
-    for l in (a, a + 1, c, c + 1):
-        if l == c:
+    for k in range(1, L):
+        if k == m:
             v.wait_ge(sem.rr4, 1)
-        if l != me:
-            v.quantize_mx(cols(T.uq, l), cols(T.up, l), share(T.hr, l)).then_inc(sem.qr, 1)
-    g.wait_ge(sem.qr, len(others))
-    scatter(raw, T.uq, T.tq, L + me, sem["tr%d" % me])
-    scatter(cols, T.up, T.tp, L + me, sem["tr%d" % me])
-    v.tensor_tensor(T.hs[:], share(T.ho, me), share(T.hr, me), AluOpType.add).then_inc(sem.hsd, 1)
+        pack(T.uq, T.up, T.hr, k, "qr")
+    g.wait_ge(sem.qr, m)
+    scatter(raw, T.uq, T.tq, L, lambda c: "tr%d" % slot(c, core))
+    scatter(cols, T.up, T.tp, L, lambda c: "tr%d" % slot(c, core))
+
+    for i, (bk, free) in enumerate([(1, "rr1"), (2, "rr2"), (3, "rr3"), (0, "rr4")]):
+        t.wait_ge(sem[free], 1)
+        product(T.mq, T.mp, i, 0, 1, bk, "pt%d" % i)
+        clamp(0, T.hr, i, 0, 1, bk, "pt%d" % i, "rt%d" % i)
+    for i in range(L):
+        v.wait_ge(sem["rs%d" % i], 1)
+        v.wait_ge(sem["rt%d" % i], 1)
+    v.tensor_tensor(T.hs[:], T.ho[:, 0:B], T.hr[:, 0:B], AluOpType.add).then_inc(sem.hsd, 1)
     v.wait_ge(sem.hsd, 1)
-    v.quantize_mx(cols(T.oq, me), cols(T.op, me), T.hs[:]).then_inc(sem.qself, 1)
+    v.quantize_mx(cols(T.oq, 0), cols(T.op, 0), T.hs[:]).then_inc(sem.qself, 1)
 
     t.wait_ge(sem.qs, L)
-    tq = [(T.tq, T.tp, l, sem.town, sum(2 * len(term_bits(mine[x])[me]) for x in others)) for l in others]
-    tq += [(T.oq, T.op, me, sem.qself, 1)]
-    late = [l for l in others if port(mine[l])] + [l for l in others if not port(mine[l])]
-    tq += [(T.tq, T.tp, L + l, sem["tr%d" % l], 2 * len(term_bits(mine[l])[me])) for l in late]
-    for k, (cq, cp, slot, s, n) in enumerate(tq):
-        t.wait_ge(s, n)
+    tq = [(T.tq, T.tp, slot(core, c), "town", sum(2 * len(term_bits(x)[core]) for x in rest(core))) for c in rest(core)]
+    tq += [(T.oq, T.op, 0, "qself", 1)]
+    for c in sorted(rest(core), key=lambda c: (not port(c), topo.die(c) != topo.die(core))):
+        tq += [(T.tq, T.tp, L + slot(core, c), "tr%d" % slot(core, c), 2 * len(term_bits(c)[core]))]
+    for k, (cq, cp, at, s, n) in enumerate(tq):
+        t.wait_ge(sem[s], n)
         for b in range(L):
-            m = t.matmul_mx(bank(T.pu, b, W), cols(T.sq, b), cols(T.sp, b), cols(cq, slot), cols(cp, slot),
-                            k == 0, k == len(tq) - 1)
+            mm = t.matmul_mx(bank(T.pu, b, 1), cols(T.sq, b), cols(T.sp, b), cols(cq, at), cols(cp, at),
+                             k == 0, k == len(tq) - 1)
             if k == len(tq) - 1:
-                m.then_inc(sem["un%d" % b], 1)
+                mm.then_inc(sem["un%d" % b], 1)
 
     for b in range(L):
-        q = (g.scalar, v)[b % 2]
-        q.wait_ge(sem["un%d" % b], 1)
+        (g.scalar, v)[b % 2].wait_ge(sem["un%d" % b], 1)
+        out, in_ = T.ys[:, b:B:4], bank(T.pu, b, 1)
         if b % 2:
-            v.tensor_copy(T.ys[:, b:4 * W:4], bank(T.pu, b, W)).then_inc(sem.yd, 1)
+            v.tensor_copy(out, in_).then_inc(sem.yd, 1)
         else:
-            g.scalar.activation(T.ys[:, b:4 * W:4], bank(T.pu, b, W), ActivationFunctionType.Copy).then_inc(sem.yd, 1)
+            g.scalar.activation(out, in_, ActivationFunctionType.Copy).then_inc(sem.yd, 1)
     g.sync.wait_ge(sem.yd, L)
     g.sync.dma_start(T.y[:], T.ys[:]).then_inc(sem.stored, 16)
     g.sync.wait_ge(sem.stored, 16)

from concourse.bass import DstId, RemoteDMATransfer
from concourse.mybir import dt, AluOpType, ActivationFunctionType

W = 128
CODES = "float8_e4m3fn_x4"
L = 4
B = 4 * W
SIM = 64

SCRATCH = {
    "lda": ("sbuf", [128, B * L], "bfloat16"),
    "ldb": ("sbuf", [128, B], "bfloat16"),
    "aq": ("sbuf", [128, L * W], CODES), "ap": ("sbuf", [128, L * W], "uint8"),
    "bq": ("sbuf", [128, L * W], CODES), "bp": ("sbuf", [128, L * W], "uint8"),
    "rq": ("sbuf", [128, L * W], CODES), "rp": ("sbuf", [128, L * W], "uint8"),
    "mq": ("sbuf", [128, L * W], CODES), "mp": ("sbuf", [128, L * W], "uint8"),
    "one": ("sbuf", [128, W], "bfloat16"),
    "eye": ("sbuf", [128, B + 4], "bfloat16"),
    "sq": ("sbuf", [128, L * W], CODES), "sp": ("sbuf", [128, L * W], "uint8"),
    "ho": ("sbuf", [128, B * L], "bfloat16"),
    "hr": ("sbuf", [128, B * L], "bfloat16"),
    "hs": ("sbuf", [128, B], "bfloat16"),
    "oq": ("sbuf", [128, L * W], CODES), "op": ("sbuf", [128, L * W], "uint8"),
    "uq": ("sbuf", [128, L * W], CODES), "up": ("sbuf", [128, L * W], "uint8"),
    "tq": ("sbuf", [128, 2 * L * W], CODES), "tp": ("sbuf", [128, 2 * L * W], "uint8"),
    "ys": ("sbuf", [128, B], "float32"),
    "pp": ("psum", [128, 512 * 4], "float32"),
    "pu": ("psum", [128, 512 * 4], "float32"),
}
FORWARDED = [(0, 1, "plane"), (1, 1, "plane"), (None, 0, "rank"), (2, 1, "rank"), (3, 1, "plane")]
DIRECT = [(0, 2, None), (2, 2, None), (None, 0, None)]
SEND_FORWARDED = ["bq", 0, 1, 2, "bp", 3, 4]
SEND_DIRECT = ["bq", 0, "bp", 1, 2]
SEMAPHORES = (["lb", "la0", "la1", "ones", "zero", "diag", "eyed", "qb", "qa0", "qa1", "qs", "barr", "sent", "qo", "qr",
               "qself", "hsd", "town", "yd", "stored", "pr4", "rr4"]
              + ["m%d" % k for k in range(5)] + ["r%d" % k for k in range(5)]
              + [p + "%d" % i for p in ("po", "ro", "ps", "rs", "pr", "rr", "pt", "rt", "tr", "un") for i in range(4)])


def rank_program(g, core, T, topo):
    homes = sorted({topo.chip(c) for c in T.cores})
    chip = topo.chip(core)
    if chip not in homes:
        homes = [x for x in homes if topo.same_plane(x, chip)] + [x for x in homes if topo.mates(x, chip)]
        if len(homes) < 2:
            return
        chip = homes[0]
    mine = [c for c in T.cores if topo.chip(c) == chip]
    far = [c for c in T.cores if topo.chip(c) != chip]
    sem = T.sem
    sent = [0]

    def rest(c):
        return [x for x in mine if x != c]

    def slot(d, s):
        return 0 if s == d else 1 + rest(d).index(s)

    def partner(c):
        return far[mine.index(c)]

    def port(c):
        return topo.may_write(c, partner(c))

    def via(c, way):
        own = [w for w in range(SIM) if topo.die(w) == topo.die(c) and topo.may_write(w, partner(c))]
        if way == "rank":
            return [w for w in own if w in mine][0]
        return [w for w in own if topo.same_plane(topo.chip(w), chip) and topo.mates(topo.chip(w), topo.chip(far[0]))][0]

    def chunks(c):
        return DIRECT if port(c) else FORWARDED

    def engines(src, dst):
        m = topo.mask(src, dst)
        return [1 << k for k in range(m.bit_length()) if m >> k & 1]

    def did(c):
        rid, pid, _ = topo.addr(c)
        return DstId(rid=rid, pnc=pid)

    def send(out, in_, rsem, dst):
        rid, pid, _ = topo.addr(dst)
        bits = engines(core, dst)
        g.remote_dma(out, in_, rsem, sem.sent, pid, rid, sum(bits))
        sent[0] += len(bits)

    def cols(t, k, n=1):
        return t[:, k * W:(k + n) * W]

    def raw(t, k, n=1):
        return t[:, k * W:(k + n) * W].bitcast(dt.uint8)

    def chunk(q, p, x):
        return cols(p, 0, L) if x[0] is None else raw(q, x[0], x[1])

    def bcast_bits(c):
        return [k for k in engines(c, rest(c)[0]) if k not in engines(c, partner(c))]

    def term_bits(s):
        e = engines(s, rest(s)[0])
        q = len(e) // 2
        away = [e[0:q:2], e[q::2]]
        return {c: e[1::2] if topo.die(c) == topo.die(s) else away.pop(0) for c in rest(s)}

    def forward():
        for s in mine:
            for k, x in enumerate(chunks(s)):
                if x[2] is not None and via(s, x[2]) == core:
                    g.wait_ge(sem["r%d" % k], len(engines(s, core)))
                    send(chunk(T.mq, T.mp, x), chunk(T.rq, T.rp, x), sem["m%d" % k], partner(s))

    if core not in mine:
        forward()
        if sent[0]:
            g.wait_ge(sem.sent, sent[0])
        return

    h = B * L // 2
    g.sync.dma_start(T.ldb[:], T.b[:]).then_inc(sem.lb, 16)
    g.sync.dma_start(T.lda[:, 0:h], T.a[:, 0:h]).then_inc(sem.la0, 16)
    g.sync.dma_start(T.lda[:, h:2 * h], T.a[:, h:2 * h]).then_inc(sem.la1, 16)

    v = g.vector
    v.memset(T.one[:], 1.0).then_inc(sem.ones, 1)
    v.memset(T.eye[:], 0.0).then_inc(sem.zero, 1)
    g.wait_ge(sem.ones, 1)
    g.affine_select(T.one[:], T.one[:], [[-1, W]], AluOpType.is_equal, 0.0, 0, 1).then_inc(sem.diag, 1)
    v.wait_ge(sem.diag, 1)
    v.wait_ge(sem.zero, 1)
    v.tensor_copy(T.eye[:, 3:3 + B:4], T.one[:]).then_inc(sem.eyed, 1)

    v.wait_ge(sem.lb, 16)
    v.quantize_mx(cols(T.bq, 0), cols(T.bp, 0), T.ldb[:]).then_inc(sem.qb, 1)
    v.wait_ge(sem.la0, 16)
    v.quantize_mx(cols(T.aq, 0, 2), cols(T.ap, 0, 2), T.lda[:, 0:h]).then_inc(sem.qa0, 1)
    v.wait_ge(sem.la1, 16)
    v.quantize_mx(cols(T.aq, 2, 2), cols(T.ap, 2, 2), T.lda[:, h:2 * h]).then_inc(sem.qa1, 1)
    v.wait_ge(sem.eyed, 1)
    for b in range(L):
        v.quantize_mx(cols(T.sq, b), cols(T.sp, b), T.eye[:, 3 - b:3 - b + B]).then_inc(sem.qs, 1)

    def bcast(view_of, buf):
        bits = bcast_bits(core)
        g.remote_dma_fused([RemoteDMATransfer(dst_ids=[did(c) for c in rest(core)], dma_engine_mask=sum(bits),
                                              remote_sem=sem.barr, srcs=[view_of(buf, 0)],
                                              dsts=[view_of(buf, slot(c, core)) for c in rest(core)])],
                           local_sem=sem.sent)
        sent[0] += len(bits)

    g.wait_ge(sem.qb, 1)
    ready = []

    def need(x):
        if x not in ready:
            g.wait_ge(sem[x], 1)
            ready.append(x)

    for step in (SEND_DIRECT if port(core) else SEND_FORWARDED):
        if step == "bp":
            bcast(cols, T.bp)
        elif step == "bq":
            bcast(raw, T.bq)
        else:
            x = chunks(core)[step]
            if x[0] is None or x[0] < 2:
                need("qa0")
            if x[0] is None or x[0] + x[1] > 2:
                need("qa1")
            if x[2] is None:
                send(chunk(T.mq, T.mp, x), chunk(T.aq, T.ap, x), sem["m%d" % step], partner(core))
            else:
                send(chunk(T.rq, T.rp, x), chunk(T.aq, T.ap, x), sem["r%d" % step], via(core, x[2]))
    forward()

    t = g.tensor

    def bank(ps, k, n):
        return ps[:, 512 * k:512 * k + n * W]

    def product(q, p, i, lo, n, bk, done):
        t.matmul_mx(bank(T.pp, bk, n), cols(q, i), cols(p, i), cols(T.bq, lo, n), cols(T.bp, lo, n), True, True
                    ).then_inc(sem[done], 1)

    def clamp(on, h, i, lo, n, bk, after, done):
        (g.scalar, v)[on].wait_ge(sem[after], 1)
        out, in_ = h[:, B * lo + i:B * (lo + n):4], bank(T.pp, bk, n)
        if on == 0:
            g.scalar.activation(out, in_, ActivationFunctionType.Relu).then_inc(sem[done], 1)
        else:
            v.tensor_scalar(out, in_, 0.0, None, AluOpType.max).then_inc(sem[done], 1)

    def pack(q, p, h, k, s):
        v.quantize_mx(cols(q, k), cols(p, k), h[:, B * k:B * (k + 1)]).then_inc(sem[s], 1)

    def scatter(view_of, src, dst, base, rsem):
        bits = term_bits(core)
        g.remote_dma_fused([RemoteDMATransfer(dst_ids=[did(c)], dma_engine_mask=sum(bits[c]), remote_sem=sem[rsem(c)],
                                              srcs=[view_of(src, slot(core, c))],
                                              dsts=[view_of(dst, base + slot(c, core))]) for c in rest(core)],
                           local_sem=sem.sent)
        sent[0] += sum(len(bits[c]) for c in rest(core))

    m = L - 1
    t.wait_ge(sem.qb, 1)
    t.wait_ge(sem.qa0, 1)
    for i in range(L):
        if i == 2:
            t.wait_ge(sem.qa1, 1)
        product(T.aq, T.ap, i, 0, 1, i, "ps%d" % i)
        clamp(0, T.ho, i, 0, 1, i, "ps%d" % i, "rs%d" % i)
    t.wait_ge(sem.barr, sum(2 * len(bcast_bits(c)) for c in rest(core)))
    for i in range(L):
        t.wait_ge(sem["rs%d" % i], 1)
        product(T.aq, T.ap, i, 1, m, i, "po%d" % i)
        clamp(i % 2, T.ho, i, 1, m, i, "po%d" % i, "ro%d" % i)
    for i in range(L):
        v.wait_ge(sem["ro%d" % i], 1)
    for k in range(1, L):
        pack(T.oq, T.op, T.ho, k, "qo")
    g.wait_ge(sem.qo, m)
    scatter(raw, T.oq, T.tq, 0, lambda c: "town")
    scatter(cols, T.op, T.tp, 0, lambda c: "town")

    s_far = partner(core)
    kinds = DIRECT if topo.may_write(s_far, core) else FORWARDED
    n_far = len(engines(s_far, core))
    got = []

    def arrived(k):
        if k not in got:
            t.wait_ge(sem["m%d" % k], n_far)
            got.append(k)

    holds = {i: k for k, x in enumerate(kinds) if x[0] is not None for i in range(x[0], x[0] + x[1])}
    arrived([k for k, x in enumerate(kinds) if x[0] is None][0])
    for k, (i, bk, lo, n, on) in enumerate([(0, 0, 1, m, 0), (1, 1, 1, m, 1), (2, 2, 1, m, 0), (3, 3, 1, 2, 1), (3, 0, 3, 1, 0)]):
        arrived(holds[i])
        t.wait_ge(sem["ro%d" % bk] if k < 4 else sem.rr0, 1)
        product(T.mq, T.mp, i, lo, n, bk, "pr%d" % k)
        clamp(on, T.hr, i, lo, n, bk, "pr%d" % k, "rr%d" % k)
    for k in range(4):
        v.wait_ge(sem["rr%d" % k], 1)
    for k in range(1, L):
        if k == m:
            v.wait_ge(sem.rr4, 1)
        pack(T.uq, T.up, T.hr, k, "qr")
    g.wait_ge(sem.qr, m)
    scatter(raw, T.uq, T.tq, L, lambda c: "tr%d" % slot(c, core))
    scatter(cols, T.up, T.tp, L, lambda c: "tr%d" % slot(c, core))

    for i, (bk, free) in enumerate([(1, "rr1"), (2, "rr2"), (3, "rr3"), (0, "rr4")]):
        t.wait_ge(sem[free], 1)
        product(T.mq, T.mp, i, 0, 1, bk, "pt%d" % i)
        clamp(0, T.hr, i, 0, 1, bk, "pt%d" % i, "rt%d" % i)
    for i in range(L):
        v.wait_ge(sem["rs%d" % i], 1)
        v.wait_ge(sem["rt%d" % i], 1)
    v.tensor_tensor(T.hs[:], T.ho[:, 0:B], T.hr[:, 0:B], AluOpType.add).then_inc(sem.hsd, 1)
    v.wait_ge(sem.hsd, 1)
    v.quantize_mx(cols(T.oq, 0), cols(T.op, 0), T.hs[:]).then_inc(sem.qself, 1)

    t.wait_ge(sem.qs, L)
    tq = [(T.tq, T.tp, slot(core, c), "town", sum(2 * len(term_bits(x)[core]) for x in rest(core))) for c in rest(core)]
    tq += [(T.oq, T.op, 0, "qself", 1)]
    for c in sorted(rest(core), key=lambda c: (not port(c), topo.die(c) != topo.die(core))):
        tq += [(T.tq, T.tp, L + slot(core, c), "tr%d" % slot(core, c), 2 * len(term_bits(c)[core]))]
    for k, (cq, cp, at, s, n) in enumerate(tq):
        t.wait_ge(sem[s], n)
        for b in range(L):
            mm = t.matmul_mx(bank(T.pu, b, 1), cols(T.sq, b), cols(T.sp, b), cols(cq, at), cols(cp, at),
                             k == 0, k == len(tq) - 1)
            if k == len(tq) - 1:
                mm.then_inc(sem["un%d" % b], 1)

    for b in range(L):
        (g.scalar, v)[b % 2].wait_ge(sem["un%d" % b], 1)
        out, in_ = T.ys[:, b:B:4], bank(T.pu, b, 1)
        if b % 2:
            v.tensor_copy(out, in_).then_inc(sem.yd, 1)
        else:
            g.scalar.activation(out, in_, ActivationFunctionType.Copy).then_inc(sem.yd, 1)
    g.sync.wait_ge(sem.yd, L)
    g.sync.dma_start(T.y[:], T.ys[:]).then_inc(sem.stored, 16)
    g.sync.wait_ge(sem.stored, 16)
    g.wait_ge(sem.sent, sent[0])
